import numpy as np
import ml_dtypes


def mxq(x, axis, fmt="e4m3"):
    dtype, down = {"e4m3": (ml_dtypes.float8_e4m3fn, 7), "e5m2": (ml_dtypes.float8_e5m2, 14)}[fmt]
    v = np.moveaxis(np.asarray(x, np.float32).astype(ml_dtypes.bfloat16).astype(np.float64), axis, -1)
    blocks = v.reshape(v.shape[:-1] + (-1, 32))
    amax = np.abs(blocks).max(-1, keepdims=True)
    byte = np.maximum(np.where(amax > 0, np.frexp(amax)[1] - 1 + 127, 0) - down, 1)
    scale = np.exp2(byte - 127.0)
    codes = (blocks / scale).astype(np.float32).astype(dtype).astype(np.float64)
    return np.moveaxis((codes * scale).reshape(v.shape), -1, axis)


WIDE = False


def mx_kscale(k):
    if not WIDE:
        return np.ones(k)
    levels = np.array([10, -10, 5, -5, 0])
    if k % 512:
        return np.exp2(np.random.permutation(np.resize(levels, k // 32))).repeat(32)
    a = np.empty((k // 512, 16))
    for p in range(k // 512):
        a[p, :8] = np.random.permutation(np.resize(levels, 8))
        for g in range(8):
            far = levels[np.abs(levels - a[p, g]) >= 10]
            a[p, g + 8] = far[np.random.randint(len(far))]
    return np.exp2(a.ravel()).repeat(32)


def f64(x):
    return np.asarray(x).astype(np.float64)


def striped(idx):
    return np.tile(idx.reshape(-1, 16).T, (8, 1)).astype(np.uint16)


def unstriped(offs):
    return offs[:16].T.reshape(-1).astype(np.int64)


def striped8(idx):
    return np.concatenate([x.reshape(-1, 16).T for x in idx]).astype(np.uint16)


def runs(offs, k):
    lists = np.stack([offs[16 * r : 16 * r + 16].T.reshape(-1) for r in range(8)]).astype(np.int64)
    return lists[np.arange(k) % 512 // 64]


def pack_weight(w):
    k, n = w.shape
    w = f64(np.asarray(w, np.float32).astype(ml_dtypes.bfloat16)).reshape(k // 32, 32, n)
    amax = np.abs(w).max(1)
    byte = np.clip(np.where(amax > 0, np.frexp(amax)[1] - 1 + 127 - 7, 1), 1, 254)
    scaled = (w * np.exp2(127.0 - byte)[:, None, :]).reshape(k, n).astype(np.float32)
    words = np.ascontiguousarray(scaled.reshape(k // 512, 128, 4, n).transpose(0, 1, 3, 2)).astype(ml_dtypes.float8_e4m3fn).view(np.uint8)
    return words, np.ascontiguousarray(byte.astype(np.uint8).reshape(k // 512, 16, n))


def unpack_weight(words, scales):
    g, p, n, _ = words.shape
    vals = np.ascontiguousarray(words).view(ml_dtypes.float8_e4m3fn).astype(np.float64) * np.repeat(np.exp2(scales.astype(np.float64) - 127.0), 8, axis=1)[..., None]
    return vals.transpose(0, 1, 3, 2).reshape(g * 512, n)


K, T, S, N, H, W = 512, 2048, 512, 512, 512, 256


def setup_inputs():
    n = np.random.standard_normal
    s = mx_kscale(K)[:, None]
    u = mx_kscale(H)
    packed_xT = pack_weight(n((K, T)) * s)
    perm = np.stack([np.random.permutation(S) for _ in range(8)])
    return {
        "x_words": packed_xT[0],
        "x_scales": packed_xT[1],
        "w1": (n((K, H)) / np.sqrt(K) / s).astype(np.float32),
        "gn": (np.random.uniform(0.5, 1.5, (H, 1)) * u[:, None]).astype(np.float32),
        "w2": (n((H, N)) / np.sqrt(H) / u[:, None]).astype(np.float32),
        "offs": striped(np.random.permutation(T)[:S]),
        "n1": striped8(perm[:, :W]),
        "n2": striped8(perm[:, W:]),
        "n3": striped8(np.stack([np.random.permutation(S) for _ in range(8)])),
        "n4": striped8(np.stack([np.random.permutation(S) for _ in range(8)])),
    }


def reference(x_words, x_scales, w1, gn, w2, offs, n1, n2, n3, n4):
    xq = unpack_weight(x_words, x_scales)[:, unstriped(offs)]
    y = mxq(f64(w1), 0, "e4m3").T @ xq
    pb = y[np.arange(H)[:, None], runs(n2, H)]
    pa = y[np.arange(H)[:, None], runs(n1, H)]
    rb = pb - (0.5 * pa)
    ra = np.sqrt((pa) ** 2 + (pb) ** 2 + 0.25)
    ds = np.zeros((H, S))
    ds[np.arange(H)[:, None], runs(n1, H)] = ra
    dt = ds.copy()
    dt[np.arange(H)[:, None], runs(n2, H)] = rb
    z = f64(gn) * dt
    h = mxq(f64(w2), 0, "e4m3").T @ mxq(z, 0, "e4m3")
    return h * (np.tanh(y[np.arange(H)[:, None], runs(n3, H)] - (y[np.arange(H)[:, None], runs(n4, H)])))

@@ -1,0 +1,157 @@
+from contextlib import ExitStack
+
+import concourse.mybir as mybir
+
+K, T, S, N, H, W = 512, 2048, 512, 512, 512, 256
+FLOPS = 2 * K * H * S + 2 * H * N * S
+
+F32 = mybir.dt.float32
+BF16 = mybir.dt.bfloat16
+I32 = mybir.dt.int32
+U32 = mybir.dt.uint32
+U16 = mybir.dt.uint16
+U8 = mybir.dt.uint8
+FP8X4 = mybir.dt.float8_e4m3fn_x4
+ALU = mybir.AluOpType
+ACT = mybir.ActivationFunctionType
+
+P = 128
+PACK = 4
+HALF = S // 2
+
+
+def tile_picked_skipjointbpolar_none_p_kernel(tc, x_words, x_scales, w1, gn, w2, offs, n1, n2, n3, n4, out):
+    nc = tc.nc
+    with ExitStack() as ctx:
+        lists = ctx.enter_context(tc.tile_pool(name="lists", bufs=1))
+        sb = ctx.enter_context(tc.tile_pool(name="sb", bufs=1))
+        psum = ctx.enter_context(tc.psum_pool(name="psum", bufs=1))
+
+        offs_sb = lists.tile([P, S // 16], U16, name="offs_sb")
+        n1_sb = lists.tile([P, W // 16], U16, name="n1_sb")
+        n2_sb = lists.tile([P, W // 16], U16, name="n2_sb")
+        n3_sb = lists.tile([P, S // 16], U16, name="n3_sb")
+        n4_sb = lists.tile([P, S // 16], U16, name="n4_sb")
+
+        table_scales = sb.tile([P, T], U8, name="table_scales", align_bytes=64)
+        table_words = sb.tile([P, T], I32, name="table_words", align_bytes=64)
+        w1_raw = sb.tile([P, PACK, H], F32, name="w1_raw")
+        w2_raw = sb.tile([P, PACK, N], F32, name="w2_raw")
+        gain = sb.tile([P, PACK], F32, name="gain")
+
+        nc.vector.memset(table_scales[:].bitcast(I32), 0)
+        nc.sync.dma_start(offs_sb[:], offs)
+        nc.sync.dma_start(w1_raw[:], w1.rearrange("(p j) c -> p j c", j=PACK))
+        for q in range(4):
+            nc.sync.dma_start(table_scales[32 * q : 32 * q + 4, :].bitcast(I32), x_scales[0, 4 * q : 4 * q + 4, :].bitcast(I32))
+        nc.sync.dma_start(table_words[:], x_words[0].rearrange("p n r -> p (n r)").bitcast(I32))
+        nc.sync.dma_start(n1_sb[:], n1)
+        nc.sync.dma_start(n2_sb[:], n2)
+        nc.sync.dma_start(w2_raw[:], w2.rearrange("(p j) c -> p j c", j=PACK))
+        nc.sync.dma_start(n4_sb[:], n4)
+        nc.sync.dma_start(n3_sb[:], n3)
+        nc.sync.dma_start(gain[:], gn.rearrange("(p t) o -> p (t o)", t=PACK))
+
+        def dealt(grouped, raw, t0, t1):
+            dst = grouped[:].rearrange("p (t m j) -> p m t j", t=PACK, j=PACK)[:, :, t0:t1, :]
+            src = raw[:].rearrange("p j (m t) -> p m t j", t=PACK)[:, :, t0:t1, :]
+            return dst, src
+
+        w1_bf = sb.tile([P, PACK * H], BF16, name="w1_bf", align_bytes=64)
+        nc.vector.tensor_copy(*dealt(w1_bf, w1_raw, 0, 3))
+        nc.scalar.copy(*dealt(w1_bf, w1_raw, 3, 4))
+
+        x_scale_g = sb.tile([P, S], U8, name="x_scale_g", align_bytes=64)
+        nc.vector.tensor_copy(x_scale_g[:], table_scales[:].indirect(offs_sb[:]))
+
+        w1_codes = sb.tile([P, H], U32, name="w1_codes", align_bytes=64)
+        w1_scale = sb.tile([P, H], U8, name="w1_scale", align_bytes=64)
+        nc.vector.quantize_mx(out=w1_codes[:].bitcast(FP8X4), scales=w1_scale[:], in_=w1_bf[:])
+
+        x_codes_g = sb.tile([P, S], U32, name="x_codes_g", align_bytes=64)
+        nc.vector.tensor_copy(x_codes_g[:], table_words[:].bitcast(U32).indirect(offs_sb[:]))
+
+        y_ps = [psum.tile([P, S], F32, name="y_ps%d" % t) for t in range(PACK)]
+        y = [sb.tile([P, S], F32, name="y%d" % t) for t in range(PACK)]
+        for t in range(PACK):
+            cols = slice(t * P, (t + 1) * P)
+            nc.tensor.matmul_mx(out=y_ps[t][:], lhsT=w1_codes[:, cols].bitcast(FP8X4), lhsT_scale=w1_scale[:, cols],
+                                rhs=x_codes_g[:].bitcast(FP8X4), rhs_scale=x_scale_g[:], start=True, stop=True)
+            nc.vector.tensor_copy(y[t][:], y_ps[t][:])
+
+        w2_bf = sb.tile([P, PACK * N], BF16, name="w2_bf", align_bytes=64)
+        dst, src = dealt(w2_bf, w2_raw, 0, 4)
+        nc.gpsimd.tensor_scalar(dst, src, 1.0, 0.0, ALU.mult, ALU.add)
+
+        pair = [sb.tile([P, 2 * W], F32, name="pair%d" % t) for t in range(PACK)]
+        dt = [sb.tile([P, S], F32, name="dt%d" % t) for t in range(PACK)]
+        sq = sb.tile([P, PACK, S], F32, name="sq")
+        for t in range(PACK):
+            nc.scalar.activation(pair[t][:, 0:W], y[t][:].indirect(n1_sb[:]), ACT.Copy, scale=-0.5)
+            nc.scalar.activation(pair[t][:, W:], y[t][:].indirect(n2_sb[:]), ACT.Copy)
+            nc.scalar.activation(dt[t][:], pair[t][:], ACT.Square)
+            nc.vector.scalar_tensor_tensor(sq[:, t, 0:W], dt[t][:, 0:W], 4.0, dt[t][:, W:], ALU.mult, ALU.add)
+            nc.vector.tensor_tensor(dt[t][:].indirect(n2_sb[:]), pair[t][:, W:], pair[t][:, 0:W], ALU.add)
+
+        ra = sb.tile([P, PACK, W], F32, name="ra")
+        nc.scalar.activation(ra[:], sq[:, :, 0:W], ACT.Sqrt, bias=0.25)
+
+        w2_codes = sb.tile([P, N], U32, name="w2_codes", align_bytes=64)
+        w2_scale = sb.tile([P, N], U8, name="w2_scale", align_bytes=64)
+        nc.vector.quantize_mx(out=w2_codes[:].bitcast(FP8X4), scales=w2_scale[:], in_=w2_bf[:])
+
+        g4 = sb.tile([P, PACK, S], F32, name="g4")
+        g3 = sb.tile([P, S], F32, name="g3")
+        z_planes = sb.tile([P, PACK, S], BF16, name="z_planes")
+        for t in range(PACK):
+            for u in range(2):
+                nc.scalar.activation(g4[:, t, u * HALF : (u + 1) * HALF], y[t][:].indirect(n4_sb[:, u * 16 : (u + 1) * 16]), ACT.Copy)
+        for u in range(2):
+            nc.scalar.activation(g3[:, u * HALF : (u + 1) * HALF], y[3][:].indirect(n3_sb[:, u * 16 : (u + 1) * 16]), ACT.Copy)
+        for t in range(PACK):
+            nc.vector.tensor_copy(dt[t][:].indirect(n1_sb[:]), ra[:, t, :])
+            if t < 3:
+                nc.scalar.activation(z_planes[:, t, :], dt[t][:], ACT.Copy, scale=gain[:, t : t + 1])
+            else:
+                nc.vector.tensor_scalar(z_planes[:, t, :], dt[t][:], gain[:, t : t + 1], None, ALU.mult)
+
+        z_bf = [sb.tile([P, HALF * PACK], BF16, name="z_bf%d" % u, align_bytes=64) for u in range(2)]
+        z_codes = sb.tile([P, S], U32, name="z_codes", align_bytes=64)
+        z_scale = sb.tile([P, S], U8, name="z_scale", align_bytes=64)
+        for u in range(2):
+            cols = slice(u * HALF, (u + 1) * HALF)
+            dst = z_bf[u][:].rearrange("p (c t) -> p c t", t=PACK)
+            src = z_planes[:, :, cols].rearrange("p t c -> p c t")
+            if u == 0:
+                nc.vector.tensor_copy(dst, src)
+            else:
+                nc.scalar.copy(dst, src)
+            nc.vector.quantize_mx(out=z_codes[:, cols].bitcast(FP8X4), scales=z_scale[:, cols], in_=z_bf[u][:])
+
+        out_rows = out.rearrange("(p t) j -> p t j", t=PACK)
+        h_ps = [psum.tile([P, S], F32, name="h_ps%d" % t) for t in range(PACK)]
+        for t in range(PACK):
+            wc = slice(t * P, (t + 1) * P)
+            nc.tensor.matmul_mx(out=h_ps[t][:], lhsT=w2_codes[:, wc].bitcast(FP8X4), lhsT_scale=w2_scale[:, wc],
+                                rhs=z_codes[:].bitcast(FP8X4), rhs_scale=z_scale[:], start=True, stop=True)
+
+        def difference(t):
+            if t < 3:
+                for u in range(2):
+                    cols = slice(u * HALF, (u + 1) * HALF)
+                    nc.vector.tensor_tensor(dt[t][:, cols], y[t][:].indirect(n3_sb[:, u * 16 : (u + 1) * 16]), g4[:, t, cols], ALU.subtract)
+            else:
+                nc.vector.tensor_tensor(dt[t][:], g3[:], g4[:, t, :], ALU.subtract)
+            nc.scalar.activation(sq[:, t, :], dt[t][:], ACT.Tanh)
+
+        def finish(t):
+            nc.vector.tensor_tensor(pair[t][:], h_ps[t][:], sq[:, t, :], ALU.mult)
+            nc.sync.dma_start(out_rows[:, t, :], pair[t][:])
+
+        difference(0)
+        difference(1)
+        difference(2)
+        finish(0)
+        difference(3)
+        for t in range(1, PACK):
+            finish(t)

@@ -41,10 +41,10 @@ def tile_picked_skipjointbpolar_none_p_kernel(tc, x_words, x_scales, w1, gn, w2,
 
         nc.vector.memset(table_scales[:].bitcast(I32), 0)
         nc.sync.dma_start(offs_sb[:], offs)
-        nc.sync.dma_start(w1_raw[:], w1.rearrange("(p j) c -> p j c", j=PACK))
+        nc.sync.dma_start(table_words[:], x_words[0].rearrange("p n r -> p (n r)").bitcast(I32))
         for q in range(4):
             nc.sync.dma_start(table_scales[32 * q : 32 * q + 4, :].bitcast(I32), x_scales[0, 4 * q : 4 * q + 4, :].bitcast(I32))
-        nc.sync.dma_start(table_words[:], x_words[0].rearrange("p n r -> p (n r)").bitcast(I32))
+        nc.sync.dma_start(w1_raw[:], w1.rearrange("(p j) c -> p j c", j=PACK))
         nc.sync.dma_start(n1_sb[:], n1)
         nc.sync.dma_start(n2_sb[:], n2)
         nc.sync.dma_start(w2_raw[:], w2.rearrange("(p j) c -> p j c", j=PACK))
@@ -57,19 +57,19 @@ def tile_picked_skipjointbpolar_none_p_kernel(tc, x_words, x_scales, w1, gn, w2,
             src = raw[:].rearrange("p j (m t) -> p m t j", t=PACK)[:, :, t0:t1, :]
             return dst, src
 
-        w1_bf = sb.tile([P, PACK * H], BF16, name="w1_bf", align_bytes=64)
-        nc.vector.tensor_copy(*dealt(w1_bf, w1_raw, 0, 3))
-        nc.scalar.copy(*dealt(w1_bf, w1_raw, 3, 4))
-
+        x_codes_g = sb.tile([P, S], U32, name="x_codes_g", align_bytes=64)
+        nc.vector.tensor_copy(x_codes_g[:], table_words[:].bitcast(U32).indirect(offs_sb[:]))
         x_scale_g = sb.tile([P, S], U8, name="x_scale_g", align_bytes=64)
         nc.vector.tensor_copy(x_scale_g[:], table_scales[:].indirect(offs_sb[:]))
 
+        w1_bf = sb.tile([P, PACK * H], BF16, name="w1_bf", align_bytes=64)
         w1_codes = sb.tile([P, H], U32, name="w1_codes", align_bytes=64)
         w1_scale = sb.tile([P, H], U8, name="w1_scale", align_bytes=64)
-        nc.vector.quantize_mx(out=w1_codes[:].bitcast(FP8X4), scales=w1_scale[:], in_=w1_bf[:])
-
-        x_codes_g = sb.tile([P, S], U32, name="x_codes_g", align_bytes=64)
-        nc.vector.tensor_copy(x_codes_g[:], table_words[:].bitcast(U32).indirect(offs_sb[:]))
+        nc.vector.tensor_copy(*dealt(w1_bf, w1_raw, 0, 2))
+        nc.scalar.copy(*dealt(w1_bf, w1_raw, 2, 4))
+        for u in range(2):
+            cols = slice(u * 2 * P, (u + 1) * 2 * P)
+            nc.vector.quantize_mx(out=w1_codes[:, cols].bitcast(FP8X4), scales=w1_scale[:, cols], in_=w1_bf[:, u * 2 * H : (u + 1) * 2 * H])
 
         y_ps = [psum.tile([P, S], F32, name="y_ps%d" % t) for t in range(PACK)]
         y = [sb.tile([P, S], F32, name="y%d" % t) for t in range(PACK)]
@@ -85,37 +85,40 @@ def tile_picked_skipjointbpolar_none_p_kernel(tc, x_words, x_scales, w1, gn, w2,
 
         pair = [sb.tile([P, 2 * W], F32, name="pair%d" % t) for t in range(PACK)]
         dt = [sb.tile([P, S], F32, name="dt%d" % t) for t in range(PACK)]
-        sq = sb.tile([P, PACK, S], F32, name="sq")
+        sums = sb.tile([P, PACK, W], F32, name="sums", tag="sums_y4")
+        scratch = sb.tile([P, PACK - 1, S], F32, name="scratch")
         for t in range(PACK):
             nc.scalar.activation(pair[t][:, 0:W], y[t][:].indirect(n1_sb[:]), ACT.Copy, scale=-0.5)
             nc.scalar.activation(pair[t][:, W:], y[t][:].indirect(n2_sb[:]), ACT.Copy)
-            nc.scalar.activation(dt[t][:], pair[t][:], ACT.Square)
-            nc.vector.scalar_tensor_tensor(sq[:, t, 0:W], dt[t][:, 0:W], 4.0, dt[t][:, W:], ALU.mult, ALU.add)
+            squares = dt[t][:] if t == 3 else scratch[:, t, :]
+            nc.scalar.activation(squares, pair[t][:], ACT.Square)
+            nc.vector.scalar_tensor_tensor(sums[:, t, :], squares[:, 0:W], 4.0, squares[:, W:], ALU.mult, ALU.add)
             nc.vector.tensor_tensor(dt[t][:].indirect(n2_sb[:]), pair[t][:, W:], pair[t][:, 0:W], ALU.add)
 
         ra = sb.tile([P, PACK, W], F32, name="ra")
-        nc.scalar.activation(ra[:], sq[:, :, 0:W], ACT.Sqrt, bias=0.25)
+        nc.scalar.activation(ra[:], sums[:], ACT.Sqrt, bias=0.25)
 
         w2_codes = sb.tile([P, N], U32, name="w2_codes", align_bytes=64)
         w2_scale = sb.tile([P, N], U8, name="w2_scale", align_bytes=64)
         nc.vector.quantize_mx(out=w2_codes[:].bitcast(FP8X4), scales=w2_scale[:], in_=w2_bf[:])
 
-        g4 = sb.tile([P, PACK, S], F32, name="g4")
-        g3 = sb.tile([P, S], F32, name="g3")
-        z_planes = sb.tile([P, PACK, S], BF16, name="z_planes")
+        def halves(lst):
+            return [(slice(u * HALF, (u + 1) * HALF), lst[:, u * 16 : (u + 1) * 16]) for u in range(2)]
+
+        y4 = sb.tile([P, PACK, S], F32, name="y4", tag="sums_y4")
+        y3 = {t: sb.tile([P, S], F32, name="y3_%d" % t) for t in (3,)}
+        z_planes = sb.tile([P, PACK, S], BF16, name="z_planes", tag="planes_tanh")
         for t in range(PACK):
-            for u in range(2):
-                nc.scalar.activation(g4[:, t, u * HALF : (u + 1) * HALF], y[t][:].indirect(n4_sb[:, u * 16 : (u + 1) * 16]), ACT.Copy)
-        for u in range(2):
-            nc.scalar.activation(g3[:, u * HALF : (u + 1) * HALF], y[3][:].indirect(n3_sb[:, u * 16 : (u + 1) * 16]), ACT.Copy)
+            for cols, offsets in halves(n4_sb):
+                nc.scalar.activation(y4[:, t, cols], y[t][:].indirect(offsets), ACT.Copy)
+            if t in y3:
+                for cols, offsets in halves(n3_sb):
+                    nc.scalar.activation(y3[t][:, cols], y[t][:].indirect(offsets), ACT.Copy)
         for t in range(PACK):
             nc.vector.tensor_copy(dt[t][:].indirect(n1_sb[:]), ra[:, t, :])
-            if t < 3:
-                nc.scalar.activation(z_planes[:, t, :], dt[t][:], ACT.Copy, scale=gain[:, t : t + 1])
-            else:
-                nc.vector.tensor_scalar(z_planes[:, t, :], dt[t][:], gain[:, t : t + 1], None, ALU.mult)
+            nc.scalar.activation(z_planes[:, t, :], dt[t][:], ACT.Copy, scale=gain[:, t : t + 1])
 
-        z_bf = [sb.tile([P, HALF * PACK], BF16, name="z_bf%d" % u, align_bytes=64) for u in range(2)]
+        z_bf = [sb.tile([P, HALF * PACK], BF16, name="z_bf%d" % u, align_bytes=64, tag="z_bf%d" % u) for u in range(2)]
         z_codes = sb.tile([P, S], U32, name="z_codes", align_bytes=64)
         z_scale = sb.tile([P, S], U8, name="z_scale", align_bytes=64)
         for u in range(2):
@@ -130,28 +133,20 @@ def tile_picked_skipjointbpolar_none_p_kernel(tc, x_words, x_scales, w1, gn, w2,
 
         out_rows = out.rearrange("(p t) j -> p t j", t=PACK)
         h_ps = [psum.tile([P, S], F32, name="h_ps%d" % t) for t in range(PACK)]
-        for t in range(PACK):
+        for t in (3, 0, 1, 2):
             wc = slice(t * P, (t + 1) * P)
             nc.tensor.matmul_mx(out=h_ps[t][:], lhsT=w2_codes[:, wc].bitcast(FP8X4), lhsT_scale=w2_scale[:, wc],
                                 rhs=z_codes[:].bitcast(FP8X4), rhs_scale=z_scale[:], start=True, stop=True)
 
-        def difference(t):
-            if t < 3:
-                for u in range(2):
-                    cols = slice(u * HALF, (u + 1) * HALF)
-                    nc.vector.tensor_tensor(dt[t][:, cols], y[t][:].indirect(n3_sb[:, u * 16 : (u + 1) * 16]), g4[:, t, cols], ALU.subtract)
+        th = sb.tile([P, PACK, S], F32, name="th", tag="planes_tanh")
+        diff = [dt[0], sb.tile([P, S], F32, name="diff_z0", align_bytes=64, tag="z_bf0"), sb.tile([P, S], F32, name="diff_z1", align_bytes=64, tag="z_bf1"), dt[3]]
+        for t in (3, 0, 1, 2):
+            if t in y3:
+                nc.vector.tensor_tensor(diff[t][:], y3[t][:], y4[:, t, :], ALU.subtract)
             else:
-                nc.vector.tensor_tensor(dt[t][:], g3[:], g4[:, t, :], ALU.subtract)
-            nc.scalar.activation(sq[:, t, :], dt[t][:], ACT.Tanh)
-
-        def finish(t):
-            nc.vector.tensor_tensor(pair[t][:], h_ps[t][:], sq[:, t, :], ALU.mult)
+                for cols, offsets in halves(n3_sb):
+                    nc.vector.tensor_tensor(diff[t][:, cols], y[t][:].indirect(offsets), y4[:, t, cols], ALU.subtract)
+            nc.scalar.activation(th[:, t, :], diff[t][:], ACT.Tanh)
+        for t in (3, 0, 1, 2):
+            nc.vector.tensor_tensor(pair[t][:], h_ps[t][:], th[:, t, :], ALU.mult)
             nc.sync.dma_start(out_rows[:, t, :], pair[t][:])
-
-        difference(0)
-        difference(1)
-        difference(2)
-        finish(0)
-        difference(3)
-        for t in range(1, PACK):
-            finish(t)

@@ -57,6 +57,10 @@ def tile_picked_skipjointbpolar_none_p_kernel(tc, x_words, x_scales, w1, gn, w2,
             src = raw[:].rearrange("p j (m t) -> p m t j", t=PACK)[:, :, t0:t1, :]
             return dst, src
 
+        warm = sb.tile([P, 1], F32, name="warm")
+        nc.gpsimd.memset(warm[:], 1.0)
+        nc.scalar.activation(warm[:], warm[:], ACT.Sqrt)
+
         x_codes_g = sb.tile([P, S], U32, name="x_codes_g", align_bytes=64)
         nc.vector.tensor_copy(x_codes_g[:], table_words[:].bitcast(U32).indirect(offs_sb[:]))
         x_scale_g = sb.tile([P, S], U8, name="x_scale_g", align_bytes=64)

from contextlib import ExitStack

import concourse.mybir as mybir

K, T, S, N, H, W = 512, 2048, 512, 512, 512, 256
FLOPS = 2 * K * H * S + 2 * H * N * S

F32 = mybir.dt.float32
BF16 = mybir.dt.bfloat16
I32 = mybir.dt.int32
U32 = mybir.dt.uint32
U16 = mybir.dt.uint16
U8 = mybir.dt.uint8
FP8X4 = mybir.dt.float8_e4m3fn_x4
ALU = mybir.AluOpType
ACT = mybir.ActivationFunctionType

P = 128
PACK = 4
HALF = S // 2


def tile_picked_skipjointbpolar_none_p_kernel(tc, x_words, x_scales, w1, gn, w2, offs, n1, n2, n3, n4, out):
    nc = tc.nc
    with ExitStack() as ctx:
        lists = ctx.enter_context(tc.tile_pool(name="lists", bufs=1))
        sb = ctx.enter_context(tc.tile_pool(name="sb", bufs=1))
        psum = ctx.enter_context(tc.psum_pool(name="psum", bufs=1))

        offs_sb = lists.tile([P, S // 16], U16, name="offs_sb")
        n1_sb = lists.tile([P, W // 16], U16, name="n1_sb")
        n2_sb = lists.tile([P, W // 16], U16, name="n2_sb")
        n3_sb = lists.tile([P, S // 16], U16, name="n3_sb")
        n4_sb = lists.tile([P, S // 16], U16, name="n4_sb")

        table_scales = sb.tile([P, T], U8, name="table_scales", align_bytes=64)
        table_words = sb.tile([P, T], I32, name="table_words", align_bytes=64)
        w1_raw = sb.tile([P, PACK, H], F32, name="w1_raw")
        w2_raw = sb.tile([P, PACK, N], F32, name="w2_raw")
        gain = sb.tile([P, PACK], F32, name="gain")

        nc.vector.memset(table_scales[:].bitcast(I32), 0)
        nc.sync.dma_start(offs_sb[:], offs)
        nc.sync.dma_start(table_words[:], x_words[0].rearrange("p n r -> p (n r)").bitcast(I32))
        for q in range(4):
            nc.sync.dma_start(table_scales[32 * q : 32 * q + 4, :].bitcast(I32), x_scales[0, 4 * q : 4 * q + 4, :].bitcast(I32))
        nc.sync.dma_start(w1_raw[:], w1.rearrange("(p j) c -> p j c", j=PACK))
        nc.sync.dma_start(n1_sb[:], n1)
        nc.sync.dma_start(n2_sb[:], n2)
        nc.sync.dma_start(w2_raw[:], w2.rearrange("(p j) c -> p j c", j=PACK))
        nc.sync.dma_start(n4_sb[:], n4)
        nc.sync.dma_start(n3_sb[:], n3)
        nc.sync.dma_start(gain[:], gn.rearrange("(p t) o -> p (t o)", t=PACK))

        def dealt(grouped, raw, t0, t1):
            dst = grouped[:].rearrange("p (t m j) -> p m t j", t=PACK, j=PACK)[:, :, t0:t1, :]
            src = raw[:].rearrange("p j (m t) -> p m t j", t=PACK)[:, :, t0:t1, :]
            return dst, src

        warm = sb.tile([P, 1], F32, name="warm")
        nc.gpsimd.memset(warm[:], 1.0)
        nc.scalar.activation(warm[:], warm[:], ACT.Sqrt)

        x_codes_g = sb.tile([P, S], U32, name="x_codes_g", align_bytes=64)
        nc.vector.tensor_copy(x_codes_g[:], table_words[:].bitcast(U32).indirect(offs_sb[:]))
        x_scale_g = sb.tile([P, S], U8, name="x_scale_g", align_bytes=64)
        nc.vector.tensor_copy(x_scale_g[:], table_scales[:].indirect(offs_sb[:]))

        w1_bf = sb.tile([P, PACK * H], BF16, name="w1_bf", align_bytes=64)
        w1_codes = sb.tile([P, H], U32, name="w1_codes", align_bytes=64)
        w1_scale = sb.tile([P, H], U8, name="w1_scale", align_bytes=64)
        nc.vector.tensor_copy(*dealt(w1_bf, w1_raw, 0, 2))
        nc.scalar.copy(*dealt(w1_bf, w1_raw, 2, 4))
        for u in range(2):
            cols = slice(u * 2 * P, (u + 1) * 2 * P)
            nc.vector.quantize_mx(out=w1_codes[:, cols].bitcast(FP8X4), scales=w1_scale[:, cols], in_=w1_bf[:, u * 2 * H : (u + 1) * 2 * H])

        y_ps = [psum.tile([P, S], F32, name="y_ps%d" % t) for t in range(PACK)]
        y = [sb.tile([P, S], F32, name="y%d" % t) for t in range(PACK)]
        for t in range(PACK):
            cols = slice(t * P, (t + 1) * P)
            nc.tensor.matmul_mx(out=y_ps[t][:], lhsT=w1_codes[:, cols].bitcast(FP8X4), lhsT_scale=w1_scale[:, cols],
                                rhs=x_codes_g[:].bitcast(FP8X4), rhs_scale=x_scale_g[:], start=True, stop=True)
            nc.vector.tensor_copy(y[t][:], y_ps[t][:])

        w2_bf = sb.tile([P, PACK * N], BF16, name="w2_bf", align_bytes=64)
        dst, src = dealt(w2_bf, w2_raw, 0, 4)
        nc.gpsimd.tensor_scalar(dst, src, 1.0, 0.0, ALU.mult, ALU.add)

        pair = [sb.tile([P, 2 * W], F32, name="pair%d" % t) for t in range(PACK)]
        dt = [sb.tile([P, S], F32, name="dt%d" % t) for t in range(PACK)]
        sums = sb.tile([P, PACK, W], F32, name="sums", tag="sums_y4")
        scratch = sb.tile([P, PACK - 1, S], F32, name="scratch")
        for t in range(PACK):
            nc.scalar.activation(pair[t][:, 0:W], y[t][:].indirect(n1_sb[:]), ACT.Copy, scale=-0.5)
            nc.scalar.activation(pair[t][:, W:], y[t][:].indirect(n2_sb[:]), ACT.Copy)
            squares = dt[t][:] if t == 3 else scratch[:, t, :]
            nc.scalar.activation(squares, pair[t][:], ACT.Square)
            nc.vector.scalar_tensor_tensor(sums[:, t, :], squares[:, 0:W], 4.0, squares[:, W:], ALU.mult, ALU.add)
            nc.vector.tensor_tensor(dt[t][:].indirect(n2_sb[:]), pair[t][:, W:], pair[t][:, 0:W], ALU.add)

        ra = sb.tile([P, PACK, W], F32, name="ra")
        nc.scalar.activation(ra[:], sums[:], ACT.Sqrt, bias=0.25)

        w2_codes = sb.tile([P, N], U32, name="w2_codes", align_bytes=64)
        w2_scale = sb.tile([P, N], U8, name="w2_scale", align_bytes=64)
        nc.vector.quantize_mx(out=w2_codes[:].bitcast(FP8X4), scales=w2_scale[:], in_=w2_bf[:])

        def halves(lst):
            return [(slice(u * HALF, (u + 1) * HALF), lst[:, u * 16 : (u + 1) * 16]) for u in range(2)]

        y4 = sb.tile([P, PACK, S], F32, name="y4", tag="sums_y4")
        y3 = {t: sb.tile([P, S], F32, name="y3_%d" % t) for t in (3,)}
        z_planes = sb.tile([P, PACK, S], BF16, name="z_planes", tag="planes_tanh")
        for t in range(PACK):
            for cols, offsets in halves(n4_sb):
                nc.scalar.activation(y4[:, t, cols], y[t][:].indirect(offsets), ACT.Copy)
            if t in y3:
                for cols, offsets in halves(n3_sb):
                    nc.scalar.activation(y3[t][:, cols], y[t][:].indirect(offsets), ACT.Copy)
        for t in range(PACK):
            nc.vector.tensor_copy(dt[t][:].indirect(n1_sb[:]), ra[:, t, :])
            nc.scalar.activation(z_planes[:, t, :], dt[t][:], ACT.Copy, scale=gain[:, t : t + 1])

        z_bf = [sb.tile([P, HALF * PACK], BF16, name="z_bf%d" % u, align_bytes=64, tag="z_bf%d" % u) for u in range(2)]
        z_codes = sb.tile([P, S], U32, name="z_codes", align_bytes=64)
        z_scale = sb.tile([P, S], U8, name="z_scale", align_bytes=64)
        for u in range(2):
            cols = slice(u * HALF, (u + 1) * HALF)
            dst = z_bf[u][:].rearrange("p (c t) -> p c t", t=PACK)
            src = z_planes[:, :, cols].rearrange("p t c -> p c t")
            if u == 0:
                nc.vector.tensor_copy(dst, src)
            else:
                nc.scalar.copy(dst, src)
            nc.vector.quantize_mx(out=z_codes[:, cols].bitcast(FP8X4), scales=z_scale[:, cols], in_=z_bf[u][:])

        out_rows = out.rearrange("(p t) j -> p t j", t=PACK)
        h_ps = [psum.tile([P, S], F32, name="h_ps%d" % t) for t in range(PACK)]
        for t in (3, 0, 1, 2):
            wc = slice(t * P, (t + 1) * P)
            nc.tensor.matmul_mx(out=h_ps[t][:], lhsT=w2_codes[:, wc].bitcast(FP8X4), lhsT_scale=w2_scale[:, wc],
                                rhs=z_codes[:].bitcast(FP8X4), rhs_scale=z_scale[:], start=True, stop=True)

        th = sb.tile([P, PACK, S], F32, name="th", tag="planes_tanh")
        diff = [dt[0], sb.tile([P, S], F32, name="diff_z0", align_bytes=64, tag="z_bf0"), sb.tile([P, S], F32, name="diff_z1", align_bytes=64, tag="z_bf1"), dt[3]]
        for t in (3, 0, 1, 2):
            if t in y3:
                nc.vector.tensor_tensor(diff[t][:], y3[t][:], y4[:, t, :], ALU.subtract)
            else:
                for cols, offsets in halves(n3_sb):
                    nc.vector.tensor_tensor(diff[t][:, cols], y[t][:].indirect(offsets), y4[:, t, cols], ALU.subtract)
            nc.scalar.activation(th[:, t, :], diff[t][:], ACT.Tanh)
        for t in (3, 0, 1, 2):
            nc.vector.tensor_tensor(pair[t][:], h_ps[t][:], th[:, t, :], ALU.mult)
            nc.sync.dma_start(out_rows[:, t, :], pair[t][:])
